import numpy as np
import ml_dtypes


def mxq(x, axis, fmt="e4m3"):
    dtype, down = {"e4m3": (ml_dtypes.float8_e4m3fn, 7), "e5m2": (ml_dtypes.float8_e5m2, 14)}[fmt]
    v = np.moveaxis(np.asarray(x, np.float32).astype(ml_dtypes.bfloat16).astype(np.float64), axis, -1)
    blocks = v.reshape(v.shape[:-1] + (-1, 32))
    amax = np.abs(blocks).max(-1, keepdims=True)
    byte = np.maximum(np.where(amax > 0, np.frexp(amax)[1] - 1 + 127, 0) - down, 1)
    scale = np.exp2(byte - 127.0)
    codes = (blocks / scale).astype(np.float32).astype(dtype).astype(np.float64)
    return np.moveaxis((codes * scale).reshape(v.shape), -1, axis)


WIDE = False


def mx_kscale(k):
    if not WIDE:
        return np.ones(k)
    levels = np.array([10, -10, 5, -5, 0])
    if k % 512:
        return np.exp2(np.random.permutation(np.resize(levels, k // 32))).repeat(32)
    a = np.empty((k // 512, 16))
    for p in range(k // 512):
        a[p, :8] = np.random.permutation(np.resize(levels, 8))
        for g in range(8):
            far = levels[np.abs(levels - a[p, g]) >= 10]
            a[p, g + 8] = far[np.random.randint(len(far))]
    return np.exp2(a.ravel()).repeat(32)


def f64(x):
    return np.asarray(x).astype(np.float64)


def striped(idx):
    return np.tile(np.asarray(idx).reshape(-1, 16).T, (8, 1)).astype(np.uint16)


def unstriped(offs):
    return offs[:16].T.reshape(-1).astype(np.int64)


E2M1 = np.array([0.0, 0.5, 1.0, 1.5, 2.0, 3.0, 4.0, 6.0, -0.0, -0.5, -1.0, -1.5, -2.0, -3.0, -4.0, -6.0])


def pack_weight(w, fmt):
    k, n = w.shape
    w = f64(np.asarray(w, np.float32).astype(ml_dtypes.bfloat16)).reshape(k // 32, 32, n)
    amax = np.abs(w).max(1)
    if fmt == "e4m3":
        byte = np.frexp(amax)[1] - 1 + 127 - 7
    else:
        mant, ex = np.frexp(amax / 6.0)
        byte = np.where(mant > 0.5, ex, ex - 1) + 127
    byte = np.clip(np.where(amax > 0, byte, 1), 1, 254)
    scaled = (w * np.exp2(127.0 - byte)[:, None, :]).reshape(k, n).astype(np.float32)
    by_word = np.ascontiguousarray(scaled.reshape(k // 512, 128, 4, n).transpose(0, 1, 3, 2))
    if fmt == "e4m3":
        words = by_word.astype(ml_dtypes.float8_e4m3fn).view(np.uint8)
    else:
        c = by_word.astype(ml_dtypes.float4_e2m1fn).view(np.uint8) & 0xF
        words = (c[..., 0::2] | (c[..., 1::2] << 4)).reshape(k // 512, 128, 2 * n)
    return np.ascontiguousarray(words), np.ascontiguousarray(byte.astype(np.uint8).reshape(k // 512, 16, n))


def unpack_weight(words, scales, fmt):
    g, _, n = scales.shape
    words = np.ascontiguousarray(words).reshape(g, 128, n, -1)
    if fmt == "e4m3":
        vals = words.view(ml_dtypes.float8_e4m3fn).astype(np.float64)
    else:
        nib = np.empty((g, 128, n, 4), np.uint8)
        nib[..., 0::2] = words & 0xF
        nib[..., 1::2] = words >> 4
        vals = E2M1[nib]
    vals = vals * np.repeat(np.exp2(scales.astype(np.float64) - 127.0), 8, axis=1)[..., None]
    return vals.transpose(0, 1, 3, 2).reshape(g * 512, n)


B, N, T, D, NQ = 1, 512, 2048, 1024, 128


def setup_inputs():
    n = np.random.standard_normal
    idx = np.random.permutation(T)[:B * N]
    s = mx_kscale(D)[:, None]
    kp = pack_weight(n((D, T)) / s, "e2m1")
    cp = pack_weight(n((D, T)) / s, "e2m1")
    return {
        "qT": (n((B, D, NQ)) * s * (1.00 / np.sqrt(D))).astype(np.float32),
        "k_words": np.ascontiguousarray(kp[0].reshape(1, 2, 128, T, 2).transpose(0, 2, 3, 1, 4)).reshape(1, 128, T, 4),
        "k_scales": kp[1],
        "c_words": np.ascontiguousarray(cp[0].reshape(1, 2, 128, T, 2).transpose(0, 2, 3, 1, 4)).reshape(1, 128, T, 4),
        "c_scales": cp[1],
        "kb": np.tile(n(2048), (128, 1)).astype(np.float32),
        "offs": striped(idx),
    }


def reference(qT, k_words, k_scales, c_words, c_scales, kb, offs):
    idx = unstriped(offs)
    pick = lambda x, which: x[:, which].reshape(x.shape[0], B, -1).transpose(1, 0, 2)
    k = unpack_weight(k_words.reshape(1, 128, T, 2, 2).transpose(0, 3, 1, 2, 4).reshape(2, 128, 2 * T), k_scales, "e2m1")
    kg = pick(k, idx)
    c = unpack_weight(c_words.reshape(1, 128, T, 2, 2).transpose(0, 3, 1, 2, 4).reshape(2, 128, 2 * T), c_scales, "e2m1")
    cg = pick(c, idx)
    qq = mxq(f64(qT), 1, "e4m3")
    a = qq.transpose(0, 2, 1) @ kg
    z = qq.transpose(0, 2, 1) @ cg
    y = np.maximum(a, z) + pick(f64(kb), idx)[:, :1, :]
    return y

@@ -1,0 +1,143 @@
+from contextlib import ExitStack
+
+import concourse.mybir as mybir
+from concourse.masks import make_identity
+
+F32 = mybir.dt.float32
+BF16 = mybir.dt.bfloat16
+I32 = mybir.dt.int32
+U32 = mybir.dt.uint32
+U16 = mybir.dt.uint16
+U8 = mybir.dt.uint8
+FP8X4 = mybir.dt.float8_e4m3fn_x4
+FP4X4 = mybir.dt.float4_e2m1fn_x4
+
+P = 128
+T = 2048
+N = 512
+NQ = 128
+PASSES = 2
+TABLES = 2
+ROW0 = 96
+HALF = N // 2
+GROUP = 128
+FLOPS = 2 * TABLES * 1024 * NQ * N
+
+
+def tile_attend_proto_topk_kernel(tc, qT, k_words, k_scales, c_words, c_scales, kb, offs, out):
+    nc = tc.nc
+    with ExitStack() as ctx:
+        pool = ctx.enter_context(tc.tile_pool(name="pool", bufs=1))
+        shared = ctx.enter_context(tc.tile_pool(name="shared", bufs=1))
+        psum = ctx.enter_context(tc.psum_pool(name="psum", bufs=1))
+
+        offsets = pool.tile([P, N // 16], U16, name="offsets")
+        nc.sync.dma_start(offsets[:], offs)
+
+        kb_win = shared.tile([P, T], F32, name="kb_win", align_bytes=64, offset=0)
+        nc.vector.memset(kb_win[:], 0.0)
+
+        scale_win = []
+        for name, scales in (("k_scale_win", k_scales), ("c_scale_win", c_scales)):
+            win = pool.tile([P, T], U8, name=name, align_bytes=64)
+            nc.vector.memset(win[0:ROW0, :].bitcast(I32), 0)
+            nc.sync.dma_start(win[ROW0:P, :].bitcast(I32), scales.rearrange("o f t -> f o t").bitcast(I32))
+            scale_win.append(win)
+
+        k_win = pool.tile([P, T], I32, name="k_win", align_bytes=64)
+        c_win = pool.tile([P, T], I32, name="c_win", align_bytes=64)
+        q_raw = pool.tile([P, PASSES, 4, NQ], F32, name="q_raw", align_bytes=64)
+        nc.sync.dma_start(k_win[:], k_words[0].rearrange("p t b -> p (t b)").bitcast(I32))
+        nc.sync.dma_start(q_raw[:], qT[0].rearrange("(o p j) w -> p o j w", o=PASSES, j=4))
+        nc.sync.dma_start(c_win[:], c_words[0].rearrange("p t b -> p (t b)").bitcast(I32))
+
+        warm_in = pool.tile([P, 1], F32, name="warm_in")
+        warm_out = pool.tile([P, 1], F32, name="warm_out")
+        nc.gpsimd.memset(warm_in[:], 0.0)
+        nc.scalar.copy(warm_out[:], warm_in[:])
+        nc.scalar.dma_start(kb_win[0:1, :], kb[0:1, :])
+
+        ident = pool.tile([P, P], F32, name="ident", align_bytes=64)
+        make_identity(nc, ident[:])
+        planes = pool.tile([P, PASSES, TABLES * N], U8, name="planes", align_bytes=64)
+        nc.gpsimd.memset(planes[:].rearrange("p o n -> p (o n)").bitcast(I32), 0)
+
+        picked_scales = pool.tile([P, TABLES, N], U8, name="picked_scales", align_bytes=64)
+        for t in range(TABLES):
+            nc.vector.tensor_copy(picked_scales[:, t, :], scale_win[t][:].indirect(offsets[:]))
+        for quad in range(4):
+            rows = slice(ROW0 + 8 * quad, ROW0 + 8 * quad + 8)
+            nc.scalar.dma_start(
+                planes[32 * quad : 32 * quad + 4].bitcast(I32),
+                picked_scales[rows].rearrange("p t n -> p (t n)").bitcast(I32),
+            )
+
+        q_bf = pool.tile([P, PASSES, NQ, 4], BF16, name="q_bf", align_bytes=64)
+        nc.scalar.copy(q_bf[:], q_raw[:].rearrange("p o j w -> p o w j"))
+
+        def gather_words(picked, win, first, count):
+            nc.vector.tensor_copy(picked[:], win[:].bitcast(U32).indirect(offsets[:, first // 16 : (first + count) // 16]))
+
+        k_picked = pool.tile([P, N], U32, name="k_picked", align_bytes=64)
+        gather_words(k_picked, k_win, 0, N)
+
+        picked_kb = pool.tile([P, N], F32, name="picked_kb", align_bytes=64)
+        nc.vector.tensor_copy(picked_kb[:], kb_win[:].indirect(offsets[:]))
+        kb_turned = psum.tile([P, N // P, P], F32, name="kb_turned")
+        for b in range(N // P):
+            nc.tensor.transpose(kb_turned[:, b, :], picked_kb[:, b * P : (b + 1) * P], ident[:])
+        kb_cols = pool.tile([P, N // P], F32, name="kb_cols", align_bytes=64)
+        nc.scalar.copy(kb_cols[:], kb_turned[:, :, 0])
+        kb_rows = psum.tile([NQ, N], F32, name="kb_rows")
+        for b in range(N // P):
+            nc.tensor.transpose(kb_rows[:, b * P : (b + 1) * P], kb_cols[:, b : b + 1].to_broadcast([P, NQ]), ident[:])
+
+        q_codes = shared.tile([P, PASSES * NQ], U32, name="q_codes", align_bytes=64, offset=0)
+        q_scales = pool.tile([P, PASSES * NQ], U8, name="q_scales", align_bytes=64)
+
+        def part_passes(name, picked, count):
+            words = pool.tile([P, PASSES, count], U16, name=name, align_bytes=64)
+            nc.vector.tensor_copy(words[:], picked[:].bitcast(U16).rearrange("p (n o) -> p o n", o=PASSES))
+            return words
+
+        def scores(dst, words, table, first, lo, count):
+            for o in range(PASSES):
+                col = table * N + first + lo
+                nc.tensor.matmul_mx(
+                    out=dst[:, lo : lo + count],
+                    lhsT=q_codes[:, o * NQ : (o + 1) * NQ].bitcast(FP8X4),
+                    lhsT_scale=q_scales[:, o * NQ : (o + 1) * NQ],
+                    rhs=words[:, o, lo : lo + count].bitcast(FP4X4),
+                    rhs_scale=planes[:, o, col : col + count],
+                    start=(o == 0),
+                    stop=(o == PASSES - 1),
+                )
+
+        k_pass = part_passes("k_pass", k_picked, N)
+        nc.vector.quantize_mx(
+            out=q_codes[:].bitcast(FP8X4),
+            scales=q_scales[:],
+            in_=q_bf[:].rearrange("p o w j -> p (o w j)"),
+        )
+        a_bank = psum.tile([NQ, N], F32, name="a_bank")
+        scores(a_bank, k_pass, 0, 0, 0, N)
+        a_sb = pool.tile([NQ, N], F32, name="a_sb", align_bytes=64)
+        nc.scalar.copy(a_sb[:], a_bank[:])
+
+        z_banks = []
+        for h in range(2):
+            c_picked = shared.tile([P, HALF], U32, name="c_picked%d" % h, align_bytes=64, offset=2048 * (h + 1))
+            gather_words(c_picked, c_win, h * HALF, HALF)
+            c_pass = part_passes("c_pass%d" % h, c_picked, HALF)
+            z_bank = psum.tile([NQ, HALF], F32, name="z_bank%d" % h)
+            for g in range(HALF // GROUP):
+                scores(z_bank, c_pass, 1, h * HALF, g * GROUP, GROUP)
+            z_banks.append(z_bank)
+
+        for h in range(2):
+            cols = slice(h * HALF, (h + 1) * HALF)
+            best = pool.tile([NQ, HALF], F32, name="best%d" % h, align_bytes=64)
+            nc.vector.tensor_tensor(best[:], z_banks[h][:], a_sb[:, cols], mybir.AluOpType.max)
+            res = pool.tile([NQ, HALF], F32, name="res%d" % h, align_bytes=64)
+            nc.vector.tensor_tensor(res[:], best[:], kb_rows[:, cols], mybir.AluOpType.add)
+            nc.sync.dma_start(out[0][:, cols], res[:])

@@ -21,6 +21,8 @@ TABLES = 2
 ROW0 = 96
 HALF = N // 2
 GROUP = 128
+RUN = T // P
+BANK_TILES = 4
 FLOPS = 2 * TABLES * 1024 * NQ * N
 
 
@@ -28,14 +30,10 @@ def tile_attend_proto_topk_kernel(tc, qT, k_words, k_scales, c_words, c_scales, 
     nc = tc.nc
     with ExitStack() as ctx:
         pool = ctx.enter_context(tc.tile_pool(name="pool", bufs=1))
-        shared = ctx.enter_context(tc.tile_pool(name="shared", bufs=1))
         psum = ctx.enter_context(tc.psum_pool(name="psum", bufs=1))
 
         offsets = pool.tile([P, N // 16], U16, name="offsets")
         nc.sync.dma_start(offsets[:], offs)
-
-        kb_win = shared.tile([P, T], F32, name="kb_win", align_bytes=64, offset=0)
-        nc.vector.memset(kb_win[:], 0.0)
 
         scale_win = []
         for name, scales in (("k_scale_win", k_scales), ("c_scale_win", c_scales)):
@@ -44,7 +42,10 @@ def tile_attend_proto_topk_kernel(tc, qT, k_words, k_scales, c_words, c_scales, 
             nc.sync.dma_start(win[ROW0:P, :].bitcast(I32), scales.rearrange("o f t -> f o t").bitcast(I32))
             scale_win.append(win)
 
-        k_win = pool.tile([P, T], I32, name="k_win", align_bytes=64)
+        kb_cols = pool.tile([P, RUN], F32, name="kb_cols", tag="chain", align_bytes=64)
+        nc.sync.dma_start(kb_cols[:], kb[0].rearrange("(p b) -> p b", b=RUN))
+
+        k_win = pool.tile([P, T], I32, name="k_win", tag="k_win", align_bytes=64)
         c_win = pool.tile([P, T], I32, name="c_win", align_bytes=64)
         q_raw = pool.tile([P, PASSES, 4, NQ], F32, name="q_raw", align_bytes=64)
         nc.sync.dma_start(k_win[:], k_words[0].rearrange("p t b -> p (t b)").bitcast(I32))
@@ -55,89 +56,90 @@ def tile_attend_proto_topk_kernel(tc, qT, k_words, k_scales, c_words, c_scales, 
         warm_out = pool.tile([P, 1], F32, name="warm_out")
         nc.gpsimd.memset(warm_in[:], 0.0)
         nc.scalar.copy(warm_out[:], warm_in[:])
-        nc.scalar.dma_start(kb_win[0:1, :], kb[0:1, :])
 
         ident = pool.tile([P, P], F32, name="ident", align_bytes=64)
         make_identity(nc, ident[:])
         planes = pool.tile([P, PASSES, TABLES * N], U8, name="planes", align_bytes=64)
         nc.gpsimd.memset(planes[:].rearrange("p o n -> p (o n)").bitcast(I32), 0)
 
+        kb_win = pool.tile([P, P, RUN], F32, name="kb_win", align_bytes=64)
+        for g in range(RUN // BANK_TILES):
+            spread = psum.tile([P, BANK_TILES, P], F32, name="spread%d" % g, tag="bank%d" % g)
+            for i in range(BANK_TILES):
+                b = g * BANK_TILES + i
+                nc.tensor.transpose(spread[:, i, :], kb_cols[:, b : b + 1].to_broadcast([P, P]), ident[:])
+            nc.scalar.copy(kb_win[:, :, g * BANK_TILES : (g + 1) * BANK_TILES], spread[:].rearrange("m i p -> m p i"))
+
         picked_scales = pool.tile([P, TABLES, N], U8, name="picked_scales", align_bytes=64)
         for t in range(TABLES):
             nc.vector.tensor_copy(picked_scales[:, t, :], scale_win[t][:].indirect(offsets[:]))
         for quad in range(4):
             rows = slice(ROW0 + 8 * quad, ROW0 + 8 * quad + 8)
-            nc.scalar.dma_start(
+            nc.sync.dma_start(
                 planes[32 * quad : 32 * quad + 4].bitcast(I32),
                 picked_scales[rows].rearrange("p t n -> p (t n)").bitcast(I32),
             )
 
-        q_bf = pool.tile([P, PASSES, NQ, 4], BF16, name="q_bf", align_bytes=64)
-        nc.scalar.copy(q_bf[:], q_raw[:].rearrange("p o j w -> p o w j"))
-
-        def gather_words(picked, win, first, count):
-            nc.vector.tensor_copy(picked[:], win[:].bitcast(U32).indirect(offsets[:, first // 16 : (first + count) // 16]))
-
-        k_picked = pool.tile([P, N], U32, name="k_picked", align_bytes=64)
-        gather_words(k_picked, k_win, 0, N)
-
-        picked_kb = pool.tile([P, N], F32, name="picked_kb", align_bytes=64)
-        nc.vector.tensor_copy(picked_kb[:], kb_win[:].indirect(offsets[:]))
-        kb_turned = psum.tile([P, N // P, P], F32, name="kb_turned")
-        for b in range(N // P):
-            nc.tensor.transpose(kb_turned[:, b, :], picked_kb[:, b * P : (b + 1) * P], ident[:])
-        kb_cols = pool.tile([P, N // P], F32, name="kb_cols", align_bytes=64)
-        nc.scalar.copy(kb_cols[:], kb_turned[:, :, 0])
-        kb_rows = psum.tile([NQ, N], F32, name="kb_rows")
-        for b in range(N // P):
-            nc.tensor.transpose(kb_rows[:, b * P : (b + 1) * P], kb_cols[:, b : b + 1].to_broadcast([P, NQ]), ident[:])
-
-        q_codes = shared.tile([P, PASSES * NQ], U32, name="q_codes", align_bytes=64, offset=0)
+        q_bf = pool.tile([P, PASSES, NQ, 4], BF16, name="q_bf", tag="chain", align_bytes=64)
+        for o in range(PASSES):
+            nc.scalar.copy(
+                q_bf[:, o].rearrange("p (c i) j -> p c j i", i=4),
+                q_raw[:, o].rearrange("p j (c i) -> p c j i", i=4),
+            )
+        q_codes = pool.tile([P, PASSES * NQ], U32, name="q_codes", align_bytes=64)
         q_scales = pool.tile([P, PASSES * NQ], U8, name="q_scales", align_bytes=64)
 
         def part_passes(name, picked, count):
             words = pool.tile([P, PASSES, count], U16, name=name, align_bytes=64)
-            nc.vector.tensor_copy(words[:], picked[:].bitcast(U16).rearrange("p (n o) -> p o n", o=PASSES))
+            nc.vector.tensor_copy(words[:], picked.bitcast(U16).rearrange("p (n o) -> p o n", o=PASSES))
             return words
 
-        def scores(dst, words, table, first, lo, count):
+        def scores(bank, words, plane_col, lo, count):
             for o in range(PASSES):
-                col = table * N + first + lo
                 nc.tensor.matmul_mx(
-                    out=dst[:, lo : lo + count],
+                    out=bank[:, lo : lo + count],
                     lhsT=q_codes[:, o * NQ : (o + 1) * NQ].bitcast(FP8X4),
                     lhsT_scale=q_scales[:, o * NQ : (o + 1) * NQ],
                     rhs=words[:, o, lo : lo + count].bitcast(FP4X4),
-                    rhs_scale=planes[:, o, col : col + count],
+                    rhs_scale=planes[:, o, plane_col + lo : plane_col + lo + count],
                     start=(o == 0),
                     stop=(o == PASSES - 1),
                 )
 
-        k_pass = part_passes("k_pass", k_picked, N)
+        k_picked = pool.tile([P, N], U32, name="k_picked", align_bytes=64)
+        nc.vector.tensor_copy(k_picked[:], k_win[:].bitcast(U32).indirect(offsets[:]))
+        k_pass = part_passes("k_pass", k_picked[:], N)
+
+        picked_kb = pool.tile([P, N], F32, name="picked_kb", tag="k_win", align_bytes=64)
+        nc.vector.tensor_copy(picked_kb[:], kb_win[:].rearrange("m p b -> m (p b)").indirect(offsets[:]))
+
         nc.vector.quantize_mx(
             out=q_codes[:].bitcast(FP8X4),
             scales=q_scales[:],
             in_=q_bf[:].rearrange("p o w j -> p (o w j)"),
         )
-        a_bank = psum.tile([NQ, N], F32, name="a_bank")
-        scores(a_bank, k_pass, 0, 0, 0, N)
-        a_sb = pool.tile([NQ, N], F32, name="a_sb", align_bytes=64)
-        nc.scalar.copy(a_sb[:], a_bank[:])
+        a_bank = psum.tile([NQ, N], F32, name="a_bank", tag="bank0")
+        scores(a_bank, k_pass, 0, 0, N)
+        a_sb = [pool.tile([NQ, HALF], F32, name="a_sb%d" % h, align_bytes=64) for h in range(2)]
+        for h in range(2):
+            nc.scalar.copy(a_sb[h][:], a_bank[:, h * HALF : (h + 1) * HALF])
 
+        c_picked = pool.tile([P, N], U32, name="c_picked", tag="chain", align_bytes=64)
         z_banks = []
         for h in range(2):
-            c_picked = shared.tile([P, HALF], U32, name="c_picked%d" % h, align_bytes=64, offset=2048 * (h + 1))
-            gather_words(c_picked, c_win, h * HALF, HALF)
-            c_pass = part_passes("c_pass%d" % h, c_picked, HALF)
-            z_bank = psum.tile([NQ, HALF], F32, name="z_bank%d" % h)
+            cols = slice(h * HALF, (h + 1) * HALF)
+            listed = offsets[:, h * HALF // 16 : (h + 1) * HALF // 16]
+            nc.vector.tensor_copy(c_picked[:, cols], c_win[:].bitcast(U32).indirect(listed))
+            c_pass = part_passes("c_pass%d" % h, c_picked[:, cols], HALF)
+            z_bank = psum.tile([NQ, HALF], F32, name="z_bank%d" % h, tag="bank%d" % (h + 1))
             for g in range(HALF // GROUP):
-                scores(z_bank, c_pass, 1, h * HALF, g * GROUP, GROUP)
+                scores(z_bank, c_pass, N + h * HALF, g * GROUP, GROUP)
             z_banks.append(z_bank)
 
         for h in range(2):
             cols = slice(h * HALF, (h + 1) * HALF)
             best = pool.tile([NQ, HALF], F32, name="best%d" % h, align_bytes=64)
-            nc.vector.tensor_tensor(best[:], z_banks[h][:], a_sb[:, cols], mybir.AluOpType.max)
+            nc.vector.tensor_tensor(best[:], z_banks[h][:], a_sb[h][:], mybir.AluOpType.max)
             res = pool.tile([NQ, HALF], F32, name="res%d" % h, align_bytes=64)
-            nc.vector.tensor_tensor(res[:], best[:], kb_rows[:, cols], mybir.AluOpType.add)
+            nc.vector.tensor_tensor(res[:], best[:], picked_kb[:, cols], mybir.AluOpType.add)
             nc.sync.dma_start(out[0][:, cols], res[:])

@@ -37,7 +37,7 @@ def tile_attend_proto_topk_kernel(tc, qT, k_words, k_scales, c_words, c_scales, 
 
         scale_win = []
         for name, scales in (("k_scale_win", k_scales), ("c_scale_win", c_scales)):
-            win = pool.tile([P, T], U8, name=name, align_bytes=64)
+            win = pool.tile([P, T], U8, name=name, tag=name, align_bytes=64)
             nc.vector.memset(win[0:ROW0, :].bitcast(I32), 0)
             nc.sync.dma_start(win[ROW0:P, :].bitcast(I32), scales.rearrange("o f t -> f o t").bitcast(I32))
             scale_win.append(win)
@@ -46,11 +46,9 @@ def tile_attend_proto_topk_kernel(tc, qT, k_words, k_scales, c_words, c_scales, 
         nc.sync.dma_start(kb_cols[:], kb[0].rearrange("(p b) -> p b", b=RUN))
 
         k_win = pool.tile([P, T], I32, name="k_win", tag="k_win", align_bytes=64)
-        c_win = pool.tile([P, T], I32, name="c_win", align_bytes=64)
         q_raw = pool.tile([P, PASSES, 4, NQ], F32, name="q_raw", align_bytes=64)
         nc.sync.dma_start(k_win[:], k_words[0].rearrange("p t b -> p (t b)").bitcast(I32))
         nc.sync.dma_start(q_raw[:], qT[0].rearrange("(o p j) w -> p o j w", o=PASSES, j=4))
-        nc.sync.dma_start(c_win[:], c_words[0].rearrange("p t b -> p (t b)").bitcast(I32))
 
         warm_in = pool.tile([P, 1], F32, name="warm_in")
         warm_out = pool.tile([P, 1], F32, name="warm_out")
@@ -73,6 +71,8 @@ def tile_attend_proto_topk_kernel(tc, qT, k_words, k_scales, c_words, c_scales, 
         picked_scales = pool.tile([P, TABLES, N], U8, name="picked_scales", align_bytes=64)
         for t in range(TABLES):
             nc.vector.tensor_copy(picked_scales[:, t, :], scale_win[t][:].indirect(offsets[:]))
+        c_win = pool.tile([P, T], I32, name="c_win", tag="k_scale_win", align_bytes=64)
+        nc.scalar.dma_start(c_win[:], c_words[0].rearrange("p t b -> p (t b)").bitcast(I32))
         for quad in range(4):
             rows = slice(ROW0 + 8 * quad, ROW0 + 8 * quad + 8)
             nc.sync.dma_start(

@@ -30,7 +30,11 @@ def tile_attend_proto_topk_kernel(tc, qT, k_words, k_scales, c_words, c_scales, 
     nc = tc.nc
     with ExitStack() as ctx:
         pool = ctx.enter_context(tc.tile_pool(name="pool", bufs=1))
+        chain = ctx.enter_context(tc.tile_pool(name="chain", bufs=1))
         psum = ctx.enter_context(tc.psum_pool(name="psum", bufs=1))
+
+        kb_cols = chain.tile([P, RUN], F32, name="kb_cols", offset=0, align_bytes=64)
+        nc.sync.dma_start(kb_cols[:], kb[0].rearrange("(p b) -> p b", b=RUN))
 
         offsets = pool.tile([P, N // 16], U16, name="offsets")
         nc.sync.dma_start(offsets[:], offs)
@@ -42,13 +46,11 @@ def tile_attend_proto_topk_kernel(tc, qT, k_words, k_scales, c_words, c_scales, 
             nc.sync.dma_start(win[ROW0:P, :].bitcast(I32), scales.rearrange("o f t -> f o t").bitcast(I32))
             scale_win.append(win)
 
-        kb_cols = pool.tile([P, RUN], F32, name="kb_cols", tag="chain", align_bytes=64)
-        nc.sync.dma_start(kb_cols[:], kb[0].rearrange("(p b) -> p b", b=RUN))
-
         k_win = pool.tile([P, T], I32, name="k_win", tag="k_win", align_bytes=64)
-        q_raw = pool.tile([P, PASSES, 4, NQ], F32, name="q_raw", align_bytes=64)
+        q_raw = [pool.tile([P, 4, NQ], F32, name="q_raw%d" % o, align_bytes=64) for o in range(PASSES)]
         nc.sync.dma_start(k_win[:], k_words[0].rearrange("p t b -> p (t b)").bitcast(I32))
-        nc.sync.dma_start(q_raw[:], qT[0].rearrange("(o p j) w -> p o j w", o=PASSES, j=4))
+        for o in range(PASSES):
+            nc.sync.dma_start(q_raw[o][:], qT[0].rearrange("(o p j) w -> o p j w", o=PASSES, j=4)[o])
 
         warm_in = pool.tile([P, 1], F32, name="warm_in")
         warm_out = pool.tile([P, 1], F32, name="warm_out")
@@ -80,11 +82,11 @@ def tile_attend_proto_topk_kernel(tc, qT, k_words, k_scales, c_words, c_scales, 
                 picked_scales[rows].rearrange("p t n -> p (t n)").bitcast(I32),
             )
 
-        q_bf = pool.tile([P, PASSES, NQ, 4], BF16, name="q_bf", tag="chain", align_bytes=64)
+        q_bf = chain.tile([P, PASSES, NQ, 4], BF16, name="q_bf", offset=0, align_bytes=64)
         for o in range(PASSES):
             nc.scalar.copy(
                 q_bf[:, o].rearrange("p (c i) j -> p c j i", i=4),
-                q_raw[:, o].rearrange("p j (c i) -> p c j i", i=4),
+                q_raw[o][:].rearrange("p j (c i) -> p c j i", i=4),
             )
         q_codes = pool.tile([P, PASSES * NQ], U32, name="q_codes", align_bytes=64)
         q_scales = pool.tile([P, PASSES * NQ], U8, name="q_scales", align_bytes=64)
@@ -106,12 +108,22 @@ def tile_attend_proto_topk_kernel(tc, qT, k_words, k_scales, c_words, c_scales, 
                     stop=(o == PASSES - 1),
                 )
 
-        k_picked = pool.tile([P, N], U32, name="k_picked", align_bytes=64)
-        nc.vector.tensor_copy(k_picked[:], k_win[:].bitcast(U32).indirect(offsets[:]))
-        k_pass = part_passes("k_pass", k_picked[:], N)
+        def listed(h):
+            return offsets[:, h * HALF // 16 : (h + 1) * HALF // 16]
 
-        picked_kb = pool.tile([P, N], F32, name="picked_kb", tag="k_win", align_bytes=64)
-        nc.vector.tensor_copy(picked_kb[:], kb_win[:].rearrange("m p b -> m (p b)").indirect(offsets[:]))
+        k_picked = [pool.tile([P, HALF], U32, name="k_picked%d" % h, tag="k_picked%d" % h, align_bytes=64) for h in range(2)]
+        for h in range(2):
+            nc.vector.tensor_copy(k_picked[h][:], k_win[:].bitcast(U32).indirect(listed(h)))
+        k_pass = pool.tile([P, PASSES, N], U16, name="k_pass", align_bytes=64)
+        for h in range(2):
+            nc.vector.tensor_copy(
+                k_pass[:, :, h * HALF : (h + 1) * HALF],
+                k_picked[h][:].bitcast(U16).rearrange("p (n o) -> p o n", o=PASSES),
+            )
+
+        kb_flat = kb_win[:].rearrange("m p b -> m (p b)")
+        picked_kb = [pool.tile([P, HALF], F32, name="picked_kb0", tag="k_picked0", align_bytes=64)]
+        nc.vector.tensor_copy(picked_kb[0][:], kb_flat.indirect(listed(0)))
 
         nc.vector.quantize_mx(
             out=q_codes[:].bitcast(FP8X4),
@@ -124,22 +136,25 @@ def tile_attend_proto_topk_kernel(tc, qT, k_words, k_scales, c_words, c_scales, 
         for h in range(2):
             nc.scalar.copy(a_sb[h][:], a_bank[:, h * HALF : (h + 1) * HALF])
 
-        c_picked = pool.tile([P, N], U32, name="c_picked", tag="chain", align_bytes=64)
+        c_picked = [
+            chain.tile([P, HALF], U32, name="c_picked%d" % h, offset=4 * HALF * h, align_bytes=64) for h in range(2)
+        ]
+        for h in range(2):
+            nc.vector.tensor_copy(c_picked[h][:], c_win[:].bitcast(U32).indirect(listed(h)))
         z_banks = []
         for h in range(2):
-            cols = slice(h * HALF, (h + 1) * HALF)
-            listed = offsets[:, h * HALF // 16 : (h + 1) * HALF // 16]
-            nc.vector.tensor_copy(c_picked[:, cols], c_win[:].bitcast(U32).indirect(listed))
-            c_pass = part_passes("c_pass%d" % h, c_picked[:, cols], HALF)
+            c_pass = part_passes("c_pass%d" % h, c_picked[h][:], HALF)
             z_bank = psum.tile([NQ, HALF], F32, name="z_bank%d" % h, tag="bank%d" % (h + 1))
             for g in range(HALF // GROUP):
                 scores(z_bank, c_pass, N + h * HALF, g * GROUP, GROUP)
             z_banks.append(z_bank)
+        picked_kb.append(chain.tile([P, HALF], F32, name="picked_kb1", offset=0, align_bytes=64))
+        nc.vector.tensor_copy(picked_kb[1][:], kb_flat.indirect(listed(1)))
 
+        best = [pool.tile([NQ, HALF], F32, name="best%d" % h, align_bytes=64) for h in range(2)]
         for h in range(2):
-            cols = slice(h * HALF, (h + 1) * HALF)
-            best = pool.tile([NQ, HALF], F32, name="best%d" % h, align_bytes=64)
-            nc.vector.tensor_tensor(best[:], z_banks[h][:], a_sb[h][:], mybir.AluOpType.max)
+            nc.vector.tensor_tensor(best[h][:], z_banks[h][:], a_sb[h][:], mybir.AluOpType.max)
+        for h in range(2):
             res = pool.tile([NQ, HALF], F32, name="res%d" % h, align_bytes=64)
-            nc.vector.tensor_tensor(res[:], best[:], picked_kb[:, cols], mybir.AluOpType.add)
-            nc.sync.dma_start(out[0][:, cols], res[:])
+            nc.vector.tensor_tensor(res[:], best[h][:], picked_kb[h][:], mybir.AluOpType.add)
+            nc.sync.dma_start(out[0][:, h * HALF : (h + 1) * HALF], res[:])

@@ -33,18 +33,18 @@ def tile_attend_proto_topk_kernel(tc, qT, k_words, k_scales, c_words, c_scales, 
         chain = ctx.enter_context(tc.tile_pool(name="chain", bufs=1))
         psum = ctx.enter_context(tc.psum_pool(name="psum", bufs=1))
 
-        kb_cols = chain.tile([P, RUN], F32, name="kb_cols", offset=0, align_bytes=64)
-        nc.sync.dma_start(kb_cols[:], kb[0].rearrange("(p b) -> p b", b=RUN))
-
         offsets = pool.tile([P, N // 16], U16, name="offsets")
         nc.sync.dma_start(offsets[:], offs)
 
         scale_win = []
-        for name, scales in (("k_scale_win", k_scales), ("c_scale_win", c_scales)):
+        for name, scales, queue in (("k_scale_win", k_scales, nc.sync), ("c_scale_win", c_scales, nc.scalar)):
             win = pool.tile([P, T], U8, name=name, tag=name, align_bytes=64)
             nc.vector.memset(win[0:ROW0, :].bitcast(I32), 0)
-            nc.sync.dma_start(win[ROW0:P, :].bitcast(I32), scales.rearrange("o f t -> f o t").bitcast(I32))
+            queue.dma_start(win[ROW0:P, :].bitcast(I32), scales.rearrange("o f t -> f o t").bitcast(I32))
             scale_win.append(win)
+
+        kb_cols = chain.tile([P, RUN], F32, name="kb_cols", offset=0, align_bytes=64)
+        nc.scalar.dma_start(kb_cols[:], kb[0].rearrange("(p b) -> p b", b=RUN))
 
         k_win = pool.tile([P, T], I32, name="k_win", tag="k_win", align_bytes=64)
         q_raw = [pool.tile([P, 4, NQ], F32, name="q_raw%d" % o, align_bytes=64) for o in range(PASSES)]
@@ -71,9 +71,9 @@ def tile_attend_proto_topk_kernel(tc, qT, k_words, k_scales, c_words, c_scales, 
             nc.scalar.copy(kb_win[:, :, g * BANK_TILES : (g + 1) * BANK_TILES], spread[:].rearrange("m i p -> m p i"))
 
         picked_scales = pool.tile([P, TABLES, N], U8, name="picked_scales", align_bytes=64)
-        for t in range(TABLES):
+        for t in reversed(range(TABLES)):
             nc.vector.tensor_copy(picked_scales[:, t, :], scale_win[t][:].indirect(offsets[:]))
-        c_win = pool.tile([P, T], I32, name="c_win", tag="k_scale_win", align_bytes=64)
+        c_win = pool.tile([P, T], I32, name="c_win", tag="c_scale_win", align_bytes=64)
         nc.scalar.dma_start(c_win[:], c_words[0].rearrange("p t b -> p (t b)").bitcast(I32))
         for quad in range(4):
             rows = slice(ROW0 + 8 * quad, ROW0 + 8 * quad + 8)
@@ -96,13 +96,13 @@ def tile_attend_proto_topk_kernel(tc, qT, k_words, k_scales, c_words, c_scales, 
             nc.vector.tensor_copy(words[:], picked.bitcast(U16).rearrange("p (n o) -> p o n", o=PASSES))
             return words
 
-        def scores(bank, words, plane_col, lo, count):
+        def scores(bank, words, first, plane_col, lo, count):
             for o in range(PASSES):
                 nc.tensor.matmul_mx(
                     out=bank[:, lo : lo + count],
                     lhsT=q_codes[:, o * NQ : (o + 1) * NQ].bitcast(FP8X4),
                     lhsT_scale=q_scales[:, o * NQ : (o + 1) * NQ],
-                    rhs=words[:, o, lo : lo + count].bitcast(FP4X4),
+                    rhs=words[:, o, lo - first : lo - first + count].bitcast(FP4X4),
                     rhs_scale=planes[:, o, plane_col + lo : plane_col + lo + count],
                     start=(o == 0),
                     stop=(o == PASSES - 1),
@@ -131,7 +131,7 @@ def tile_attend_proto_topk_kernel(tc, qT, k_words, k_scales, c_words, c_scales, 
             in_=q_bf[:].rearrange("p o w j -> p (o w j)"),
         )
         a_bank = psum.tile([NQ, N], F32, name="a_bank", tag="bank0")
-        scores(a_bank, k_pass, 0, 0, N)
+        scores(a_bank, k_pass, 0, 0, 0, N)
         a_sb = [pool.tile([NQ, HALF], F32, name="a_sb%d" % h, align_bytes=64) for h in range(2)]
         for h in range(2):
             nc.scalar.copy(a_sb[h][:], a_bank[:, h * HALF : (h + 1) * HALF])
@@ -143,10 +143,12 @@ def tile_attend_proto_topk_kernel(tc, qT, k_words, k_scales, c_words, c_scales, 
             nc.vector.tensor_copy(c_picked[h][:], c_win[:].bitcast(U32).indirect(listed(h)))
         z_banks = []
         for h in range(2):
-            c_pass = part_passes("c_pass%d" % h, c_picked[h][:], HALF)
             z_bank = psum.tile([NQ, HALF], F32, name="z_bank%d" % h, tag="bank%d" % (h + 1))
-            for g in range(HALF // GROUP):
-                scores(z_bank, c_pass, N + h * HALF, g * GROUP, GROUP)
+            width = GROUP if h == 0 else HALF
+            for first in range(0, HALF, width):
+                c_pass = part_passes("c_pass%d_%d" % (h, first), c_picked[h][:, first : first + width], width)
+                for lo in range(first, first + width, GROUP):
+                    scores(z_bank, c_pass, first, N + h * HALF, lo, GROUP)
             z_banks.append(z_bank)
         picked_kb.append(chain.tile([P, HALF], F32, name="picked_kb1", offset=0, align_bytes=64))
         nc.vector.tensor_copy(picked_kb[1][:], kb_flat.indirect(listed(1)))

@@ -33,6 +33,9 @@ def tile_attend_proto_topk_kernel(tc, qT, k_words, k_scales, c_words, c_scales, 
         chain = ctx.enter_context(tc.tile_pool(name="chain", bufs=1))
         psum = ctx.enter_context(tc.psum_pool(name="psum", bufs=1))
 
+        kb_cols = chain.tile([P, RUN], F32, name="kb_cols", offset=0, align_bytes=64)
+        nc.scalar.dma_start(kb_cols[:], kb[0].rearrange("(p b) -> p b", b=RUN))
+
         offsets = pool.tile([P, N // 16], U16, name="offsets")
         nc.sync.dma_start(offsets[:], offs)
 
@@ -43,14 +46,14 @@ def tile_attend_proto_topk_kernel(tc, qT, k_words, k_scales, c_words, c_scales, 
             queue.dma_start(win[ROW0:P, :].bitcast(I32), scales.rearrange("o f t -> f o t").bitcast(I32))
             scale_win.append(win)
 
-        kb_cols = chain.tile([P, RUN], F32, name="kb_cols", offset=0, align_bytes=64)
-        nc.scalar.dma_start(kb_cols[:], kb[0].rearrange("(p b) -> p b", b=RUN))
-
         k_win = pool.tile([P, T], I32, name="k_win", tag="k_win", align_bytes=64)
         q_raw = [pool.tile([P, 4, NQ], F32, name="q_raw%d" % o, align_bytes=64) for o in range(PASSES)]
         nc.sync.dma_start(k_win[:], k_words[0].rearrange("p t b -> p (t b)").bitcast(I32))
         for o in range(PASSES):
             nc.sync.dma_start(q_raw[o][:], qT[0].rearrange("(o p j) w -> o p j w", o=PASSES, j=4)[o])
+
+        c_win = pool.tile([P, T], I32, name="c_win", align_bytes=64)
+        nc.sync.dma_start(c_win[:], c_words[0].rearrange("p t b -> p (t b)").bitcast(I32))
 
         warm_in = pool.tile([P, 1], F32, name="warm_in")
         warm_out = pool.tile([P, 1], F32, name="warm_out")
@@ -71,10 +74,8 @@ def tile_attend_proto_topk_kernel(tc, qT, k_words, k_scales, c_words, c_scales, 
             nc.scalar.copy(kb_win[:, :, g * BANK_TILES : (g + 1) * BANK_TILES], spread[:].rearrange("m i p -> m p i"))
 
         picked_scales = pool.tile([P, TABLES, N], U8, name="picked_scales", align_bytes=64)
-        for t in reversed(range(TABLES)):
+        for t in range(TABLES):
             nc.vector.tensor_copy(picked_scales[:, t, :], scale_win[t][:].indirect(offsets[:]))
-        c_win = pool.tile([P, T], I32, name="c_win", tag="c_scale_win", align_bytes=64)
-        nc.scalar.dma_start(c_win[:], c_words[0].rearrange("p t b -> p (t b)").bitcast(I32))
         for quad in range(4):
             rows = slice(ROW0 + 8 * quad, ROW0 + 8 * quad + 8)
             nc.sync.dma_start(

@@ -18,12 +18,15 @@ N = 512
 NQ = 128
 PASSES = 2
 TABLES = 2
-ROW0 = 96
-HALF = N // 2
+PACK = 4
+QUADS = 4
+SCALE_ROW0 = 96
+HALVES = 2
+HALF = N // HALVES
 GROUP = 128
 RUN = T // P
 BANK_TILES = 4
-FLOPS = 2 * TABLES * 1024 * NQ * N
+FLOPS = 2 * TABLES * PASSES * PACK * P * NQ * N
 
 
 def tile_attend_proto_topk_kernel(tc, qT, k_words, k_scales, c_words, c_scales, kb, offs, out):
@@ -42,23 +45,18 @@ def tile_attend_proto_topk_kernel(tc, qT, k_words, k_scales, c_words, c_scales, 
         scale_win = []
         for name, scales, queue in (("k_scale_win", k_scales, nc.sync), ("c_scale_win", c_scales, nc.scalar)):
             win = pool.tile([P, T], U8, name=name, tag=name, align_bytes=64)
-            nc.vector.memset(win[0:ROW0, :].bitcast(I32), 0)
-            queue.dma_start(win[ROW0:P, :].bitcast(I32), scales.rearrange("o f t -> f o t").bitcast(I32))
+            nc.vector.memset(win[0:SCALE_ROW0, :].bitcast(I32), 0)
+            queue.dma_start(win[SCALE_ROW0:P, :].bitcast(I32), scales.rearrange("o f t -> f o t").bitcast(I32))
             scale_win.append(win)
 
         k_win = pool.tile([P, T], I32, name="k_win", tag="k_win", align_bytes=64)
-        q_raw = [pool.tile([P, 4, NQ], F32, name="q_raw%d" % o, align_bytes=64) for o in range(PASSES)]
+        q_raw = [pool.tile([P, PACK, NQ], F32, name="q_raw%d" % o, align_bytes=64) for o in range(PASSES)]
         nc.sync.dma_start(k_win[:], k_words[0].rearrange("p t b -> p (t b)").bitcast(I32))
         for o in range(PASSES):
-            nc.sync.dma_start(q_raw[o][:], qT[0].rearrange("(o p j) w -> o p j w", o=PASSES, j=4)[o])
+            nc.sync.dma_start(q_raw[o][:], qT[0].rearrange("(o p j) w -> o p j w", o=PASSES, j=PACK)[o])
 
         c_win = pool.tile([P, T], I32, name="c_win", align_bytes=64)
         nc.sync.dma_start(c_win[:], c_words[0].rearrange("p t b -> p (t b)").bitcast(I32))
-
-        warm_in = pool.tile([P, 1], F32, name="warm_in")
-        warm_out = pool.tile([P, 1], F32, name="warm_out")
-        nc.gpsimd.memset(warm_in[:], 0.0)
-        nc.scalar.copy(warm_out[:], warm_in[:])
 
         ident = pool.tile([P, P], F32, name="ident", align_bytes=64)
         make_identity(nc, ident[:])
@@ -76,14 +74,14 @@ def tile_attend_proto_topk_kernel(tc, qT, k_words, k_scales, c_words, c_scales, 
         picked_scales = pool.tile([P, TABLES, N], U8, name="picked_scales", align_bytes=64)
         for t in range(TABLES):
             nc.vector.tensor_copy(picked_scales[:, t, :], scale_win[t][:].indirect(offsets[:]))
-        for quad in range(4):
-            rows = slice(ROW0 + 8 * quad, ROW0 + 8 * quad + 8)
+        for quad in range(QUADS):
+            rows = slice(SCALE_ROW0 + 8 * quad, SCALE_ROW0 + 8 * quad + 8)
             nc.sync.dma_start(
                 planes[32 * quad : 32 * quad + 4].bitcast(I32),
                 picked_scales[rows].rearrange("p t n -> p (t n)").bitcast(I32),
             )
 
-        q_bf = chain.tile([P, PASSES, NQ, 4], BF16, name="q_bf", offset=0, align_bytes=64)
+        q_bf = chain.tile([P, PASSES, NQ, PACK], BF16, name="q_bf", offset=0, align_bytes=64)
         for o in range(PASSES):
             nc.scalar.copy(
                 q_bf[:, o].rearrange("p (c i) j -> p c j i", i=4),
@@ -92,19 +90,18 @@ def tile_attend_proto_topk_kernel(tc, qT, k_words, k_scales, c_words, c_scales, 
         q_codes = pool.tile([P, PASSES * NQ], U32, name="q_codes", align_bytes=64)
         q_scales = pool.tile([P, PASSES * NQ], U8, name="q_scales", align_bytes=64)
 
-        def part_passes(name, picked, count):
-            words = pool.tile([P, PASSES, count], U16, name=name, align_bytes=64)
-            nc.vector.tensor_copy(words[:], picked.bitcast(U16).rearrange("p (n o) -> p o n", o=PASSES))
-            return words
+        def part_passes(target, picked):
+            nc.vector.tensor_copy(target, picked.bitcast(U16).rearrange("p (n o) -> p o n", o=PASSES))
 
-        def scores(bank, words, first, plane_col, lo, count):
+        def scores(target, words, table, slot0):
+            plane0 = table * N + slot0
             for o in range(PASSES):
                 nc.tensor.matmul_mx(
-                    out=bank[:, lo : lo + count],
+                    out=target,
                     lhsT=q_codes[:, o * NQ : (o + 1) * NQ].bitcast(FP8X4),
                     lhsT_scale=q_scales[:, o * NQ : (o + 1) * NQ],
-                    rhs=words[:, o, lo - first : lo - first + count].bitcast(FP4X4),
-                    rhs_scale=planes[:, o, plane_col + lo : plane_col + lo + count],
+                    rhs=words[:, o, :].bitcast(FP4X4),
+                    rhs_scale=planes[:, o, plane0 : plane0 + words.shape[2]],
                     start=(o == 0),
                     stop=(o == PASSES - 1),
                 )
@@ -112,15 +109,18 @@ def tile_attend_proto_topk_kernel(tc, qT, k_words, k_scales, c_words, c_scales, 
         def listed(h):
             return offsets[:, h * HALF // 16 : (h + 1) * HALF // 16]
 
-        k_picked = [pool.tile([P, HALF], U32, name="k_picked%d" % h, tag="k_picked%d" % h, align_bytes=64) for h in range(2)]
-        for h in range(2):
+        def half_cols(h):
+            return slice(h * HALF, (h + 1) * HALF)
+
+        k_picked = [
+            pool.tile([P, HALF], U32, name="k_picked%d" % h, tag="k_picked%d" % h, align_bytes=64)
+            for h in range(HALVES)
+        ]
+        for h in range(HALVES):
             nc.vector.tensor_copy(k_picked[h][:], k_win[:].bitcast(U32).indirect(listed(h)))
         k_pass = pool.tile([P, PASSES, N], U16, name="k_pass", align_bytes=64)
-        for h in range(2):
-            nc.vector.tensor_copy(
-                k_pass[:, :, h * HALF : (h + 1) * HALF],
-                k_picked[h][:].bitcast(U16).rearrange("p (n o) -> p o n", o=PASSES),
-            )
+        for h in range(HALVES):
+            part_passes(k_pass[:, :, half_cols(h)], k_picked[h][:])
 
         kb_flat = kb_win[:].rearrange("m p b -> m (p b)")
         picked_kb = [pool.tile([P, HALF], F32, name="picked_kb0", tag="k_picked0", align_bytes=64)]
@@ -132,32 +132,34 @@ def tile_attend_proto_topk_kernel(tc, qT, k_words, k_scales, c_words, c_scales, 
             in_=q_bf[:].rearrange("p o w j -> p (o w j)"),
         )
         a_bank = psum.tile([NQ, N], F32, name="a_bank", tag="bank0")
-        scores(a_bank, k_pass, 0, 0, 0, N)
-        a_sb = [pool.tile([NQ, HALF], F32, name="a_sb%d" % h, align_bytes=64) for h in range(2)]
-        for h in range(2):
-            nc.scalar.copy(a_sb[h][:], a_bank[:, h * HALF : (h + 1) * HALF])
+        scores(a_bank[:], k_pass[:], 0, 0)
+        a_sb = [pool.tile([NQ, HALF], F32, name="a_sb%d" % h, align_bytes=64) for h in range(HALVES)]
+        for h in range(HALVES):
+            nc.scalar.copy(a_sb[h][:], a_bank[:, half_cols(h)])
 
         c_picked = [
-            chain.tile([P, HALF], U32, name="c_picked%d" % h, offset=4 * HALF * h, align_bytes=64) for h in range(2)
+            chain.tile([P, HALF], U32, name="c_picked%d" % h, offset=4 * HALF * h, align_bytes=64)
+            for h in range(HALVES)
         ]
-        for h in range(2):
+        for h in range(HALVES):
             nc.vector.tensor_copy(c_picked[h][:], c_win[:].bitcast(U32).indirect(listed(h)))
         z_banks = []
-        for h in range(2):
+        for h, width in enumerate((GROUP, HALF)):
             z_bank = psum.tile([NQ, HALF], F32, name="z_bank%d" % h, tag="bank%d" % (h + 1))
-            width = GROUP if h == 0 else HALF
             for first in range(0, HALF, width):
-                c_pass = part_passes("c_pass%d_%d" % (h, first), c_picked[h][:, first : first + width], width)
-                for lo in range(first, first + width, GROUP):
-                    scores(z_bank, c_pass, first, N + h * HALF, lo, GROUP)
+                c_pass = pool.tile([P, PASSES, width], U16, name="c_pass%d_%d" % (h, first), align_bytes=64)
+                part_passes(c_pass[:], c_picked[h][:, first : first + width])
+                for lo in range(0, width, GROUP):
+                    slot = first + lo
+                    scores(z_bank[:, slot : slot + GROUP], c_pass[:, :, lo : lo + GROUP], 1, h * HALF + slot)
             z_banks.append(z_bank)
         picked_kb.append(chain.tile([P, HALF], F32, name="picked_kb1", offset=0, align_bytes=64))
         nc.vector.tensor_copy(picked_kb[1][:], kb_flat.indirect(listed(1)))
 
-        best = [pool.tile([NQ, HALF], F32, name="best%d" % h, align_bytes=64) for h in range(2)]
-        for h in range(2):
+        best = [pool.tile([NQ, HALF], F32, name="best%d" % h, align_bytes=64) for h in range(HALVES)]
+        for h in range(HALVES):
             nc.vector.tensor_tensor(best[h][:], z_banks[h][:], a_sb[h][:], mybir.AluOpType.max)
-        for h in range(2):
+        for h in range(HALVES):
             res = pool.tile([NQ, HALF], F32, name="res%d" % h, align_bytes=64)
             nc.vector.tensor_tensor(res[:], best[h][:], picked_kb[h][:], mybir.AluOpType.add)
-            nc.sync.dma_start(out[0][:, h * HALF : (h + 1) * HALF], res[:])
+            nc.sync.dma_start(out[0][:, half_cols(h)], res[:])

@@ -131,6 +131,16 @@ def tile_attend_proto_topk_kernel(tc, qT, k_words, k_scales, c_words, c_scales, 
             scales=q_scales[:],
             in_=q_bf[:].rearrange("p o w j -> p (o w j)"),
         )
+        warm_bank = psum.tile([NQ, N], F32, name="warm_bank", tag="bank4")
+        nc.tensor.matmul_mx(
+            out=warm_bank[:],
+            lhsT=q_codes[:, 0:NQ].bitcast(FP8X4),
+            lhsT_scale=q_scales[:, 0:NQ],
+            rhs=k_pass[:, 0, :].bitcast(FP4X4),
+            rhs_scale=picked_scales[:, 0, :],
+            start=True,
+            stop=True,
+        )
         a_bank = psum.tile([NQ, N], F32, name="a_bank", tag="bank0")
         scores(a_bank[:], k_pass[:], 0, 0)
         a_sb = [pool.tile([NQ, HALF], F32, name="a_sb%d" % h, align_bytes=64) for h in range(HALVES)]

@@ -25,6 +25,7 @@ HALVES = 2
 HALF = N // HALVES
 GROUP = 128
 RUN = T // P
+Q_BF_BYTES = PASSES * NQ * PACK * 2
 BANK_TILES = 4
 FLOPS = 2 * TABLES * PASSES * PACK * P * NQ * N
 
@@ -36,7 +37,7 @@ def tile_attend_proto_topk_kernel(tc, qT, k_words, k_scales, c_words, c_scales, 
         chain = ctx.enter_context(tc.tile_pool(name="chain", bufs=1))
         psum = ctx.enter_context(tc.psum_pool(name="psum", bufs=1))
 
-        kb_cols = chain.tile([P, RUN], F32, name="kb_cols", offset=0, align_bytes=64)
+        kb_cols = chain.tile([P, RUN], F32, name="kb_cols", offset=Q_BF_BYTES - 32)
         nc.scalar.dma_start(kb_cols[:], kb[0].rearrange("(p b) -> p b", b=RUN))
 
         offsets = pool.tile([P, N // 16], U16, name="offsets")
@@ -50,7 +51,7 @@ def tile_attend_proto_topk_kernel(tc, qT, k_words, k_scales, c_words, c_scales, 
             scale_win.append(win)
 
         k_win = pool.tile([P, T], I32, name="k_win", tag="k_win", align_bytes=64)
-        q_raw = [pool.tile([P, PACK, NQ], F32, name="q_raw%d" % o, align_bytes=64) for o in range(PASSES)]
+        q_raw = [pool.tile([P, PACK, NQ], F32, name="q_raw%d" % o, tag="q_raw%d" % o, align_bytes=64) for o in range(PASSES)]
         nc.sync.dma_start(k_win[:], k_words[0].rearrange("p t b -> p (t b)").bitcast(I32))
         for o in range(PASSES):
             nc.sync.dma_start(q_raw[o][:], qT[0].rearrange("(o p j) w -> o p j w", o=PASSES, j=PACK)[o])
@@ -60,8 +61,6 @@ def tile_attend_proto_topk_kernel(tc, qT, k_words, k_scales, c_words, c_scales, 
 
         ident = pool.tile([P, P], F32, name="ident", align_bytes=64)
         make_identity(nc, ident[:])
-        planes = pool.tile([P, PASSES, TABLES * N], U8, name="planes", align_bytes=64)
-        nc.gpsimd.memset(planes[:].rearrange("p o n -> p (o n)").bitcast(I32), 0)
 
         kb_win = pool.tile([P, P, RUN], F32, name="kb_win", align_bytes=64)
         for g in range(RUN // BANK_TILES):
@@ -71,12 +70,15 @@ def tile_attend_proto_topk_kernel(tc, qT, k_words, k_scales, c_words, c_scales, 
                 nc.tensor.transpose(spread[:, i, :], kb_cols[:, b : b + 1].to_broadcast([P, P]), ident[:])
             nc.scalar.copy(kb_win[:, :, g * BANK_TILES : (g + 1) * BANK_TILES], spread[:].rearrange("m i p -> m p i"))
 
+        planes = chain.tile([P, PASSES, TABLES * N], U8, name="planes", offset=Q_BF_BYTES, align_bytes=64)
+        nc.gpsimd.memset(planes[:].rearrange("p o n -> p (o n)").bitcast(I32), 0)
+
         picked_scales = pool.tile([P, TABLES, N], U8, name="picked_scales", align_bytes=64)
         for t in range(TABLES):
             nc.vector.tensor_copy(picked_scales[:, t, :], scale_win[t][:].indirect(offsets[:]))
-        for quad in range(QUADS):
+        for quad in (0, 2, 1, 3):
             rows = slice(SCALE_ROW0 + 8 * quad, SCALE_ROW0 + 8 * quad + 8)
-            nc.sync.dma_start(
+            nc.scalar.dma_start(
                 planes[32 * quad : 32 * quad + 4].bitcast(I32),
                 picked_scales[rows].rearrange("p t n -> p (t n)").bitcast(I32),
             )
@@ -123,23 +125,13 @@ def tile_attend_proto_topk_kernel(tc, qT, k_words, k_scales, c_words, c_scales, 
             part_passes(k_pass[:, :, half_cols(h)], k_picked[h][:])
 
         kb_flat = kb_win[:].rearrange("m p b -> m (p b)")
-        picked_kb = [pool.tile([P, HALF], F32, name="picked_kb0", tag="k_picked0", align_bytes=64)]
-        nc.vector.tensor_copy(picked_kb[0][:], kb_flat.indirect(listed(0)))
+        picked_kb = pool.tile([P, N], F32, name="picked_kb", tag="q_raw1", align_bytes=64)
+        nc.scalar.activation(picked_kb[:], kb_flat.indirect(offsets[:]), mybir.ActivationFunctionType.Copy)
 
         nc.vector.quantize_mx(
             out=q_codes[:].bitcast(FP8X4),
             scales=q_scales[:],
             in_=q_bf[:].rearrange("p o w j -> p (o w j)"),
-        )
-        warm_bank = psum.tile([NQ, N], F32, name="warm_bank", tag="bank4")
-        nc.tensor.matmul_mx(
-            out=warm_bank[:],
-            lhsT=q_codes[:, 0:NQ].bitcast(FP8X4),
-            lhsT_scale=q_scales[:, 0:NQ],
-            rhs=k_pass[:, 0, :].bitcast(FP4X4),
-            rhs_scale=picked_scales[:, 0, :],
-            start=True,
-            stop=True,
         )
         a_bank = psum.tile([NQ, N], F32, name="a_bank", tag="bank0")
         scores(a_bank[:], k_pass[:], 0, 0)
@@ -154,22 +146,21 @@ def tile_attend_proto_topk_kernel(tc, qT, k_words, k_scales, c_words, c_scales, 
         for h in range(HALVES):
             nc.vector.tensor_copy(c_picked[h][:], c_win[:].bitcast(U32).indirect(listed(h)))
         z_banks = []
-        for h, width in enumerate((GROUP, HALF)):
-            z_bank = psum.tile([NQ, HALF], F32, name="z_bank%d" % h, tag="bank%d" % (h + 1))
-            for first in range(0, HALF, width):
-                c_pass = pool.tile([P, PASSES, width], U16, name="c_pass%d_%d" % (h, first), align_bytes=64)
-                part_passes(c_pass[:], c_picked[h][:, first : first + width])
-                for lo in range(0, width, GROUP):
-                    slot = first + lo
-                    scores(z_bank[:, slot : slot + GROUP], c_pass[:, :, lo : lo + GROUP], 1, h * HALF + slot)
+        pieces = [slice(0, HALF), slice(HALF, HALF + GROUP), slice(HALF + GROUP, N)]
+        for i, cols in enumerate(pieces):
+            z_bank = psum.tile([NQ, cols.stop - cols.start], F32, name="z_bank%d" % i, tag="bank%d" % (i + 1))
+            for first in range(cols.start, cols.stop, GROUP):
+                c_pass = pool.tile([P, PASSES, GROUP], U16, name="c_pass%d" % first, align_bytes=64)
+                part_passes(c_pass[:], c_picked[first // HALF][:, first % HALF : first % HALF + GROUP])
+                scores(z_bank[:, first - cols.start : first - cols.start + GROUP], c_pass[:], 1, first)
             z_banks.append(z_bank)
-        picked_kb.append(chain.tile([P, HALF], F32, name="picked_kb1", offset=0, align_bytes=64))
-        nc.vector.tensor_copy(picked_kb[1][:], kb_flat.indirect(listed(1)))
 
         best = [pool.tile([NQ, HALF], F32, name="best%d" % h, align_bytes=64) for h in range(HALVES)]
-        for h in range(HALVES):
-            nc.vector.tensor_tensor(best[h][:], z_banks[h][:], a_sb[h][:], mybir.AluOpType.max)
+        for i, cols in enumerate(pieces):
+            h = cols.start // HALF
+            within = slice(cols.start - h * HALF, cols.stop - h * HALF)
+            nc.vector.tensor_tensor(best[h][:, within], z_banks[i][:], a_sb[h][:, within], mybir.AluOpType.max)
         for h in range(HALVES):
             res = pool.tile([NQ, HALF], F32, name="res%d" % h, align_bytes=64)
-            nc.vector.tensor_tensor(res[:], best[h][:], picked_kb[h][:], mybir.AluOpType.add)
+            nc.vector.tensor_tensor(res[:], best[h][:], picked_kb[:, half_cols(h)], mybir.AluOpType.add)
             nc.sync.dma_start(out[0][:, half_cols(h)], res[:])

@@ -24,8 +24,8 @@ SCALE_ROW0 = 96
 HALVES = 2
 HALF = N // HALVES
 GROUP = 128
+GROUPS = N // GROUP
 RUN = T // P
-Q_BF_BYTES = PASSES * NQ * PACK * 2
 BANK_TILES = 4
 FLOPS = 2 * TABLES * PASSES * PACK * P * NQ * N
 
@@ -37,7 +37,7 @@ def tile_attend_proto_topk_kernel(tc, qT, k_words, k_scales, c_words, c_scales, 
         chain = ctx.enter_context(tc.tile_pool(name="chain", bufs=1))
         psum = ctx.enter_context(tc.psum_pool(name="psum", bufs=1))
 
-        kb_cols = chain.tile([P, RUN], F32, name="kb_cols", offset=Q_BF_BYTES - 32)
+        kb_cols = chain.tile([P, RUN], F32, name="kb_cols", offset=0, align_bytes=64)
         nc.scalar.dma_start(kb_cols[:], kb[0].rearrange("(p b) -> p b", b=RUN))
 
         offsets = pool.tile([P, N // 16], U16, name="offsets")
@@ -61,6 +61,8 @@ def tile_attend_proto_topk_kernel(tc, qT, k_words, k_scales, c_words, c_scales, 
 
         ident = pool.tile([P, P], F32, name="ident", align_bytes=64)
         make_identity(nc, ident[:])
+        planes = pool.tile([P, PASSES, TABLES * N], U8, name="planes", align_bytes=64)
+        nc.gpsimd.memset(planes[:].rearrange("p o n -> p (o n)").bitcast(I32), 0)
 
         kb_win = pool.tile([P, P, RUN], F32, name="kb_win", align_bytes=64)
         for g in range(RUN // BANK_TILES):
@@ -70,15 +72,12 @@ def tile_attend_proto_topk_kernel(tc, qT, k_words, k_scales, c_words, c_scales, 
                 nc.tensor.transpose(spread[:, i, :], kb_cols[:, b : b + 1].to_broadcast([P, P]), ident[:])
             nc.scalar.copy(kb_win[:, :, g * BANK_TILES : (g + 1) * BANK_TILES], spread[:].rearrange("m i p -> m p i"))
 
-        planes = chain.tile([P, PASSES, TABLES * N], U8, name="planes", offset=Q_BF_BYTES, align_bytes=64)
-        nc.gpsimd.memset(planes[:].rearrange("p o n -> p (o n)").bitcast(I32), 0)
-
         picked_scales = pool.tile([P, TABLES, N], U8, name="picked_scales", align_bytes=64)
         for t in range(TABLES):
             nc.vector.tensor_copy(picked_scales[:, t, :], scale_win[t][:].indirect(offsets[:]))
-        for quad in (0, 2, 1, 3):
+        for quad in range(QUADS):
             rows = slice(SCALE_ROW0 + 8 * quad, SCALE_ROW0 + 8 * quad + 8)
-            nc.scalar.dma_start(
+            nc.sync.dma_start(
                 planes[32 * quad : 32 * quad + 4].bitcast(I32),
                 picked_scales[rows].rearrange("p t n -> p (t n)").bitcast(I32),
             )
@@ -133,11 +132,11 @@ def tile_attend_proto_topk_kernel(tc, qT, k_words, k_scales, c_words, c_scales, 
             scales=q_scales[:],
             in_=q_bf[:].rearrange("p o w j -> p (o w j)"),
         )
-        a_bank = psum.tile([NQ, N], F32, name="a_bank", tag="bank0")
-        scores(a_bank[:], k_pass[:], 0, 0)
         a_sb = [pool.tile([NQ, HALF], F32, name="a_sb%d" % h, align_bytes=64) for h in range(HALVES)]
         for h in range(HALVES):
-            nc.scalar.copy(a_sb[h][:], a_bank[:, half_cols(h)])
+            a_bank = psum.tile([NQ, HALF], F32, name="a_bank%d" % h, tag="a_bank%d" % h)
+            scores(a_bank[:], k_pass[:, :, half_cols(h)], 0, h * HALF)
+            nc.scalar.copy(a_sb[h][:], a_bank[:])
 
         c_picked = [
             chain.tile([P, HALF], U32, name="c_picked%d" % h, offset=4 * HALF * h, align_bytes=64)
@@ -146,21 +145,32 @@ def tile_attend_proto_topk_kernel(tc, qT, k_words, k_scales, c_words, c_scales, 
         for h in range(HALVES):
             nc.vector.tensor_copy(c_picked[h][:], c_win[:].bitcast(U32).indirect(listed(h)))
         z_banks = []
-        pieces = [slice(0, HALF), slice(HALF, HALF + GROUP), slice(HALF + GROUP, N)]
-        for i, cols in enumerate(pieces):
-            z_bank = psum.tile([NQ, cols.stop - cols.start], F32, name="z_bank%d" % i, tag="bank%d" % (i + 1))
-            for first in range(cols.start, cols.stop, GROUP):
-                c_pass = pool.tile([P, PASSES, GROUP], U16, name="c_pass%d" % first, align_bytes=64)
-                part_passes(c_pass[:], c_picked[first // HALF][:, first % HALF : first % HALF + GROUP])
-                scores(z_bank[:, first - cols.start : first - cols.start + GROUP], c_pass[:], 1, first)
-            z_banks.append(z_bank)
+        for g in range(GROUPS):
+            c_pass = pool.tile([P, PASSES, GROUP], U16, name="c_pass%d" % g, align_bytes=64)
+            first = g * GROUP % HALF
+            part_passes(c_pass[:], c_picked[g * GROUP // HALF][:, first : first + GROUP])
+            z_banks.append(psum.tile([NQ, GROUP], F32, name="z_bank%d" % g, tag="bank%d" % (g + 1)))
+            scores(z_banks[g][:], c_pass[:], 1, g * GROUP)
 
-        best = [pool.tile([NQ, HALF], F32, name="best%d" % h, align_bytes=64) for h in range(HALVES)]
-        for i, cols in enumerate(pieces):
-            h = cols.start // HALF
-            within = slice(cols.start - h * HALF, cols.stop - h * HALF)
-            nc.vector.tensor_tensor(best[h][:, within], z_banks[i][:], a_sb[h][:, within], mybir.AluOpType.max)
-        for h in range(HALVES):
-            res = pool.tile([NQ, HALF], F32, name="res%d" % h, align_bytes=64)
-            nc.vector.tensor_tensor(res[:], best[h][:], picked_kb[:, half_cols(h)], mybir.AluOpType.add)
-            nc.sync.dma_start(out[0][:, half_cols(h)], res[:])
+        best = pool.tile([NQ, N], F32, name="best", align_bytes=64)
+
+        def larger(g):
+            first = g * GROUP % HALF
+            first_scores = a_sb[g * GROUP // HALF][:, first : first + GROUP]
+            nc.vector.tensor_tensor(
+                best[:, g * GROUP : (g + 1) * GROUP], z_banks[g][:], first_scores, mybir.AluOpType.max
+            )
+
+        def biased(first, last):
+            cols = slice(first * GROUP, (last + 1) * GROUP)
+            res = pool.tile([NQ, cols.stop - cols.start], F32, name="res%d" % first, align_bytes=64)
+            nc.vector.tensor_tensor(res[:], best[:, cols], picked_kb[:, cols], mybir.AluOpType.add)
+            nc.sync.dma_start(out[0][:, cols], res[:])
+
+        larger(0)
+        larger(1)
+        biased(0, 0)
+        larger(2)
+        larger(3)
+        biased(1, 2)
+        biased(3, 3)

@@ -124,8 +124,13 @@ def tile_attend_proto_topk_kernel(tc, qT, k_words, k_scales, c_words, c_scales, 
             part_passes(k_pass[:, :, half_cols(h)], k_picked[h][:])
 
         kb_flat = kb_win[:].rearrange("m p b -> m (p b)")
-        picked_kb = pool.tile([P, N], F32, name="picked_kb", tag="q_raw1", align_bytes=64)
-        nc.scalar.activation(picked_kb[:], kb_flat.indirect(offsets[:]), mybir.ActivationFunctionType.Copy)
+        picked_kb = [
+            pool.tile([P, HALF], F32, name="picked_kb0", tag="k_picked0", align_bytes=64),
+            pool.tile([P, HALF], F32, name="picked_kb1", tag="q_raw1", align_bytes=64),
+        ]
+        nc.vector.tensor_copy(picked_kb[0][:], kb_flat.indirect(listed(0)))
+        nc.scalar.activation(picked_kb[1][:], kb_flat.indirect(listed(1)), mybir.ActivationFunctionType.Copy)
+        kb_groups = [half[:, lo : lo + GROUP] for half in (picked_kb[0][:], picked_kb[1][:]) for lo in (0, GROUP)]
 
         nc.vector.quantize_mx(
             out=q_codes[:].bitcast(FP8X4),
@@ -161,16 +166,16 @@ def tile_attend_proto_topk_kernel(tc, qT, k_words, k_scales, c_words, c_scales, 
                 best[:, g * GROUP : (g + 1) * GROUP], z_banks[g][:], first_scores, mybir.AluOpType.max
             )
 
-        def biased(first, last):
-            cols = slice(first * GROUP, (last + 1) * GROUP)
-            res = pool.tile([NQ, cols.stop - cols.start], F32, name="res%d" % first, align_bytes=64)
-            nc.vector.tensor_tensor(res[:], best[:, cols], picked_kb[:, cols], mybir.AluOpType.add)
+        def biased(g):
+            cols = slice(g * GROUP, (g + 1) * GROUP)
+            res = pool.tile([NQ, GROUP], F32, name="res%d" % g, align_bytes=64)
+            nc.vector.tensor_tensor(res[:], best[:, cols], kb_groups[g], mybir.AluOpType.add)
             nc.sync.dma_start(out[0][:, cols], res[:])
 
         larger(0)
         larger(1)
-        biased(0, 0)
+        biased(0)
         larger(2)
         larger(3)
-        biased(1, 2)
-        biased(3, 3)
+        for g in range(1, GROUPS):
+            biased(g)

@@ -26,6 +26,10 @@ HALF = N // HALVES
 GROUP = 128
 GROUPS = N // GROUP
 RUN = T // P
+Q_BF_BYTES = 2 * NQ * PACK
+Q_RAW_BYTES = 4 * NQ * PACK
+Q_BF_AT = (Q_BF_BYTES, 3 * Q_BF_BYTES // 2)
+Q_RAW_AT = 3 * Q_BF_BYTES
 BANK_TILES = 4
 FLOPS = 2 * TABLES * PASSES * PACK * P * NQ * N
 
@@ -37,7 +41,7 @@ def tile_attend_proto_topk_kernel(tc, qT, k_words, k_scales, c_words, c_scales, 
         chain = ctx.enter_context(tc.tile_pool(name="chain", bufs=1))
         psum = ctx.enter_context(tc.psum_pool(name="psum", bufs=1))
 
-        kb_cols = chain.tile([P, RUN], F32, name="kb_cols", offset=0, align_bytes=64)
+        kb_cols = chain.tile([P, RUN], F32, name="kb_cols", offset=Q_BF_AT[0], align_bytes=64)
         nc.scalar.dma_start(kb_cols[:], kb[0].rearrange("(p b) -> p b", b=RUN))
 
         offsets = pool.tile([P, N // 16], U16, name="offsets")
@@ -51,13 +55,16 @@ def tile_attend_proto_topk_kernel(tc, qT, k_words, k_scales, c_words, c_scales, 
             scale_win.append(win)
 
         k_win = pool.tile([P, T], I32, name="k_win", tag="k_win", align_bytes=64)
-        q_raw = [pool.tile([P, PACK, NQ], F32, name="q_raw%d" % o, tag="q_raw%d" % o, align_bytes=64) for o in range(PASSES)]
-        nc.sync.dma_start(k_win[:], k_words[0].rearrange("p t b -> p (t b)").bitcast(I32))
-        for o in range(PASSES):
-            nc.sync.dma_start(q_raw[o][:], qT[0].rearrange("(o p j) w -> o p j w", o=PASSES, j=PACK)[o])
-
         c_win = pool.tile([P, T], I32, name="c_win", align_bytes=64)
+        q_raw = [
+            chain.tile([P, PACK, NQ], F32, name="q_raw%d" % o, offset=Q_RAW_AT + Q_RAW_BYTES * o, align_bytes=64)
+            for o in range(PASSES)
+        ]
+        q_passes = qT[0].rearrange("(o p j) w -> o p j w", o=PASSES, j=PACK)
+        nc.sync.dma_start(k_win[:], k_words[0].rearrange("p t b -> p (t b)").bitcast(I32))
+        nc.sync.dma_start(q_raw[0][:], q_passes[0])
         nc.sync.dma_start(c_win[:], c_words[0].rearrange("p t b -> p (t b)").bitcast(I32))
+        nc.sync.dma_start(q_raw[1][:], q_passes[1])
 
         ident = pool.tile([P, P], F32, name="ident", align_bytes=64)
         make_identity(nc, ident[:])
@@ -82,100 +89,109 @@ def tile_attend_proto_topk_kernel(tc, qT, k_words, k_scales, c_words, c_scales, 
                 picked_scales[rows].rearrange("p t n -> p (t n)").bitcast(I32),
             )
 
-        q_bf = chain.tile([P, PASSES, NQ, PACK], BF16, name="q_bf", offset=0, align_bytes=64)
-        for o in range(PASSES):
-            nc.scalar.copy(
-                q_bf[:, o].rearrange("p (c i) j -> p c j i", i=4),
-                q_raw[o][:].rearrange("p j (c i) -> p c j i", i=4),
-            )
+        q_bf = [
+            chain.tile([P, NQ, PACK], BF16, name="q_bf%d" % o, offset=Q_BF_AT[o], align_bytes=64)
+            for o in range(PASSES)
+        ]
         q_codes = pool.tile([P, PASSES * NQ], U32, name="q_codes", align_bytes=64)
         q_scales = pool.tile([P, PASSES * NQ], U8, name="q_scales", align_bytes=64)
+
+        def round_q(copy, o, queries):
+            copy(
+                q_bf[o][:, queries].rearrange("p (c i) j -> p c j i", i=4),
+                q_raw[o][:, :, queries].rearrange("p j (c i) -> p c j i", i=4),
+            )
+
+        def quantize(o):
+            nc.vector.quantize_mx(
+                out=q_codes[:, o * NQ : (o + 1) * NQ].bitcast(FP8X4),
+                scales=q_scales[:, o * NQ : (o + 1) * NQ],
+                in_=q_bf[o][:].rearrange("p w j -> p (w j)"),
+            )
 
         def part_passes(target, picked):
             nc.vector.tensor_copy(target, picked.bitcast(U16).rearrange("p (n o) -> p o n", o=PASSES))
 
-        def scores(target, words, table, slot0):
-            plane0 = table * N + slot0
-            for o in range(PASSES):
-                nc.tensor.matmul_mx(
-                    out=target,
-                    lhsT=q_codes[:, o * NQ : (o + 1) * NQ].bitcast(FP8X4),
-                    lhsT_scale=q_scales[:, o * NQ : (o + 1) * NQ],
-                    rhs=words[:, o, :].bitcast(FP4X4),
-                    rhs_scale=planes[:, o, plane0 : plane0 + words.shape[2]],
-                    start=(o == 0),
-                    stop=(o == PASSES - 1),
-                )
+        def score_pass(target, words, table, g, o):
+            plane0 = table * N + g * GROUP
+            nc.tensor.matmul_mx(
+                out=target,
+                lhsT=q_codes[:, o * NQ : (o + 1) * NQ].bitcast(FP8X4),
+                lhsT_scale=q_scales[:, o * NQ : (o + 1) * NQ],
+                rhs=words[:, o, g * GROUP : (g + 1) * GROUP].bitcast(FP4X4),
+                rhs_scale=planes[:, o, plane0 : plane0 + GROUP],
+                start=(o == 0),
+                stop=(o == PASSES - 1),
+            )
 
-        def listed(h):
-            return offsets[:, h * HALF // 16 : (h + 1) * HALF // 16]
+        def listed(first, width):
+            return offsets[:, first // 16 : (first + width) // 16]
 
         def half_cols(h):
             return slice(h * HALF, (h + 1) * HALF)
 
-        k_picked = [
-            pool.tile([P, HALF], U32, name="k_picked%d" % h, tag="k_picked%d" % h, align_bytes=64)
-            for h in range(HALVES)
-        ]
+        def group_cols(g):
+            return slice(g * GROUP, (g + 1) * GROUP)
+
+        round_q(nc.scalar.copy, 0, slice(0, NQ))
+        k_picked = [pool.tile([P, HALF], U32, name="k_picked%d" % h, align_bytes=64) for h in range(HALVES)]
         for h in range(HALVES):
-            nc.vector.tensor_copy(k_picked[h][:], k_win[:].bitcast(U32).indirect(listed(h)))
+            nc.vector.tensor_copy(k_picked[h][:], k_win[:].bitcast(U32).indirect(listed(h * HALF, HALF)))
         k_pass = pool.tile([P, PASSES, N], U16, name="k_pass", align_bytes=64)
         for h in range(HALVES):
             part_passes(k_pass[:, :, half_cols(h)], k_picked[h][:])
+        quantize(0)
 
         kb_flat = kb_win[:].rearrange("m p b -> m (p b)")
-        picked_kb = [
-            pool.tile([P, HALF], F32, name="picked_kb0", tag="k_picked0", align_bytes=64),
-            pool.tile([P, HALF], F32, name="picked_kb1", tag="q_raw1", align_bytes=64),
-        ]
-        nc.vector.tensor_copy(picked_kb[0][:], kb_flat.indirect(listed(0)))
-        nc.scalar.activation(picked_kb[1][:], kb_flat.indirect(listed(1)), mybir.ActivationFunctionType.Copy)
-        kb_groups = [half[:, lo : lo + GROUP] for half in (picked_kb[0][:], picked_kb[1][:]) for lo in (0, GROUP)]
+        picked_kb = []
 
-        nc.vector.quantize_mx(
-            out=q_codes[:].bitcast(FP8X4),
-            scales=q_scales[:],
-            in_=q_bf[:].rearrange("p o w j -> p (o w j)"),
-        )
-        a_sb = [pool.tile([NQ, HALF], F32, name="a_sb%d" % h, align_bytes=64) for h in range(HALVES)]
-        for h in range(HALVES):
-            a_bank = psum.tile([NQ, HALF], F32, name="a_bank%d" % h, tag="a_bank%d" % h)
-            scores(a_bank[:], k_pass[:, :, half_cols(h)], 0, h * HALF)
-            nc.scalar.copy(a_sb[h][:], a_bank[:])
-
-        c_picked = [
-            chain.tile([P, HALF], U32, name="c_picked%d" % h, offset=4 * HALF * h, align_bytes=64)
-            for h in range(HALVES)
-        ]
-        for h in range(HALVES):
-            nc.vector.tensor_copy(c_picked[h][:], c_win[:].bitcast(U32).indirect(listed(h)))
-        z_banks = []
-        for g in range(GROUPS):
-            c_pass = pool.tile([P, PASSES, GROUP], U16, name="c_pass%d" % g, align_bytes=64)
-            first = g * GROUP % HALF
-            part_passes(c_pass[:], c_picked[g * GROUP // HALF][:, first : first + GROUP])
-            z_banks.append(psum.tile([NQ, GROUP], F32, name="z_bank%d" % g, tag="bank%d" % (g + 1)))
-            scores(z_banks[g][:], c_pass[:], 1, g * GROUP)
-
-        best = pool.tile([NQ, N], F32, name="best", align_bytes=64)
-
-        def larger(g):
-            first = g * GROUP % HALF
-            first_scores = a_sb[g * GROUP // HALF][:, first : first + GROUP]
-            nc.vector.tensor_tensor(
-                best[:, g * GROUP : (g + 1) * GROUP], z_banks[g][:], first_scores, mybir.AluOpType.max
+        def gather_kb(h):
+            at = Q_RAW_AT + Q_RAW_BYTES * h + Q_RAW_BYTES // 2
+            picked_kb.append(chain.tile([P, HALF], F32, name="picked_kb%d" % h, offset=at, align_bytes=64))
+            nc.scalar.activation(
+                picked_kb[h][:], kb_flat.indirect(listed(h * HALF, HALF)), mybir.ActivationFunctionType.Copy
             )
 
-        def biased(g):
-            cols = slice(g * GROUP, (g + 1) * GROUP)
-            res = pool.tile([NQ, GROUP], F32, name="res%d" % g, align_bytes=64)
-            nc.vector.tensor_tensor(res[:], best[:, cols], kb_groups[g], mybir.AluOpType.add)
-            nc.sync.dma_start(out[0][:, cols], res[:])
+        c_picked = []
 
-        larger(0)
-        larger(1)
-        biased(0)
-        larger(2)
-        larger(3)
-        for g in range(1, GROUPS):
-            biased(g)
+        def gather_c(h, at):
+            c_picked.append(chain.tile([P, HALF], U32, name="c_picked%d" % h, offset=at, align_bytes=64))
+            for lo in range(0, HALF, GROUP):
+                nc.vector.tensor_copy(
+                    c_picked[h][:, lo : lo + GROUP], c_win[:].bitcast(U32).indirect(listed(h * HALF + lo, GROUP))
+                )
+
+        c_pass = pool.tile([P, PASSES, N], U16, name="c_pass", align_bytes=64)
+        gather_kb(0)
+        gather_c(0, Q_BF_BYTES // 2)
+        round_q(nc.scalar.copy, 1, slice(0, NQ // 2))
+        round_q(nc.vector.tensor_copy, 1, slice(NQ // 2, NQ))
+        part_passes(c_pass[:, :, half_cols(0)], c_picked[0][:])
+        quantize(1)
+        gather_kb(1)
+        gather_c(1, Q_RAW_AT + Q_RAW_BYTES)
+        for lo in range(0, HALF, GROUP):
+            part_passes(c_pass[:, :, HALF + lo : HALF + lo + GROUP], c_picked[1][:, lo : lo + GROUP])
+
+        a_banks = [psum.tile([NQ, GROUP], F32, name="a_bank%d" % g, tag="bank%d" % g) for g in range(GROUPS)]
+        z_banks = [psum.tile([NQ, GROUP], F32, name="z_bank%d" % g, tag="z_bank%d" % g) for g in range(GROUPS)]
+        a_sb = [pool.tile([NQ, GROUP], F32, name="a_sb%d" % g, align_bytes=64) for g in range(GROUPS)]
+        for g in range(GROUPS):
+            score_pass(a_banks[g][:], k_pass, 0, g, 0)
+        for pair in ((0, 1), (2, 3)):
+            for g in pair:
+                score_pass(a_banks[g][:], k_pass, 0, g, 1)
+                nc.scalar.copy(a_sb[g][:], a_banks[g][:])
+            for g in pair:
+                for o in range(PASSES):
+                    score_pass(z_banks[g][:], c_pass, 1, g, o)
+
+        best = pool.tile([NQ, N], F32, name="best", align_bytes=64)
+        for h, pair in enumerate(((0, 1), (2, 3))):
+            for g in pair:
+                nc.vector.tensor_tensor(best[:, group_cols(g)], z_banks[g][:], a_sb[g][:], mybir.AluOpType.max)
+            for g in pair:
+                res = pool.tile([NQ, GROUP], F32, name="res%d" % g, align_bytes=64)
+                bias = picked_kb[h][:, group_cols(g % 2)]
+                nc.vector.tensor_tensor(res[:], best[:, group_cols(g)], bias, mybir.AluOpType.add)
+                nc.sync.dma_start(out[0][:, group_cols(g)], res[:])

from contextlib import ExitStack

import concourse.mybir as mybir
from concourse.masks import make_identity

F32 = mybir.dt.float32
BF16 = mybir.dt.bfloat16
I32 = mybir.dt.int32
U32 = mybir.dt.uint32
U16 = mybir.dt.uint16
U8 = mybir.dt.uint8
FP8X4 = mybir.dt.float8_e4m3fn_x4
FP4X4 = mybir.dt.float4_e2m1fn_x4

P = 128
T = 2048
N = 512
NQ = 128
PASSES = 2
TABLES = 2
PACK = 4
QUADS = 4
SCALE_ROW0 = 96
HALVES = 2
HALF = N // HALVES
GROUP = 128
GROUPS = N // GROUP
RUN = T // P
Q_BF_BYTES = 2 * NQ * PACK
Q_RAW_BYTES = 4 * NQ * PACK
Q_BF_AT = (Q_BF_BYTES, 3 * Q_BF_BYTES // 2)
Q_RAW_AT = 3 * Q_BF_BYTES
BANK_TILES = 4
FLOPS = 2 * TABLES * PASSES * PACK * P * NQ * N


def tile_attend_proto_topk_kernel(tc, qT, k_words, k_scales, c_words, c_scales, kb, offs, out):
    nc = tc.nc
    with ExitStack() as ctx:
        pool = ctx.enter_context(tc.tile_pool(name="pool", bufs=1))
        chain = ctx.enter_context(tc.tile_pool(name="chain", bufs=1))
        psum = ctx.enter_context(tc.psum_pool(name="psum", bufs=1))

        kb_cols = chain.tile([P, RUN], F32, name="kb_cols", offset=Q_BF_AT[0], align_bytes=64)
        nc.scalar.dma_start(kb_cols[:], kb[0].rearrange("(p b) -> p b", b=RUN))

        offsets = pool.tile([P, N // 16], U16, name="offsets")
        nc.sync.dma_start(offsets[:], offs)

        scale_win = []
        for name, scales, queue in (("k_scale_win", k_scales, nc.sync), ("c_scale_win", c_scales, nc.scalar)):
            win = pool.tile([P, T], U8, name=name, tag=name, align_bytes=64)
            nc.vector.memset(win[0:SCALE_ROW0, :].bitcast(I32), 0)
            queue.dma_start(win[SCALE_ROW0:P, :].bitcast(I32), scales.rearrange("o f t -> f o t").bitcast(I32))
            scale_win.append(win)

        k_win = pool.tile([P, T], I32, name="k_win", tag="k_win", align_bytes=64)
        c_win = pool.tile([P, T], I32, name="c_win", align_bytes=64)
        q_raw = [
            chain.tile([P, PACK, NQ], F32, name="q_raw%d" % o, offset=Q_RAW_AT + Q_RAW_BYTES * o, align_bytes=64)
            for o in range(PASSES)
        ]
        q_passes = qT[0].rearrange("(o p j) w -> o p j w", o=PASSES, j=PACK)
        nc.sync.dma_start(k_win[:], k_words[0].rearrange("p t b -> p (t b)").bitcast(I32))
        nc.sync.dma_start(q_raw[0][:], q_passes[0])
        nc.sync.dma_start(c_win[:], c_words[0].rearrange("p t b -> p (t b)").bitcast(I32))
        nc.sync.dma_start(q_raw[1][:], q_passes[1])

        ident = pool.tile([P, P], F32, name="ident", align_bytes=64)
        make_identity(nc, ident[:])
        planes = pool.tile([P, PASSES, TABLES * N], U8, name="planes", align_bytes=64)
        nc.gpsimd.memset(planes[:].rearrange("p o n -> p (o n)").bitcast(I32), 0)

        kb_win = pool.tile([P, P, RUN], F32, name="kb_win", align_bytes=64)
        for g in range(RUN // BANK_TILES):
            spread = psum.tile([P, BANK_TILES, P], F32, name="spread%d" % g, tag="bank%d" % g)
            for i in range(BANK_TILES):
                b = g * BANK_TILES + i
                nc.tensor.transpose(spread[:, i, :], kb_cols[:, b : b + 1].to_broadcast([P, P]), ident[:])
            nc.scalar.copy(kb_win[:, :, g * BANK_TILES : (g + 1) * BANK_TILES], spread[:].rearrange("m i p -> m p i"))

        picked_scales = pool.tile([P, TABLES, N], U8, name="picked_scales", align_bytes=64)
        for t in range(TABLES):
            nc.vector.tensor_copy(picked_scales[:, t, :], scale_win[t][:].indirect(offsets[:]))
        for quad in range(QUADS):
            rows = slice(SCALE_ROW0 + 8 * quad, SCALE_ROW0 + 8 * quad + 8)
            nc.sync.dma_start(
                planes[32 * quad : 32 * quad + 4].bitcast(I32),
                picked_scales[rows].rearrange("p t n -> p (t n)").bitcast(I32),
            )

        q_bf = [
            chain.tile([P, NQ, PACK], BF16, name="q_bf%d" % o, offset=Q_BF_AT[o], align_bytes=64)
            for o in range(PASSES)
        ]
        q_codes = pool.tile([P, PASSES * NQ], U32, name="q_codes", align_bytes=64)
        q_scales = pool.tile([P, PASSES * NQ], U8, name="q_scales", align_bytes=64)

        def round_q(copy, o, queries):
            copy(
                q_bf[o][:, queries].rearrange("p (c i) j -> p c j i", i=4),
                q_raw[o][:, :, queries].rearrange("p j (c i) -> p c j i", i=4),
            )

        def quantize(o):
            nc.vector.quantize_mx(
                out=q_codes[:, o * NQ : (o + 1) * NQ].bitcast(FP8X4),
                scales=q_scales[:, o * NQ : (o + 1) * NQ],
                in_=q_bf[o][:].rearrange("p w j -> p (w j)"),
            )

        def part_passes(target, picked):
            nc.vector.tensor_copy(target, picked.bitcast(U16).rearrange("p (n o) -> p o n", o=PASSES))

        def score_pass(target, words, table, g, o):
            plane0 = table * N + g * GROUP
            nc.tensor.matmul_mx(
                out=target,
                lhsT=q_codes[:, o * NQ : (o + 1) * NQ].bitcast(FP8X4),
                lhsT_scale=q_scales[:, o * NQ : (o + 1) * NQ],
                rhs=words[:, o, g * GROUP : (g + 1) * GROUP].bitcast(FP4X4),
                rhs_scale=planes[:, o, plane0 : plane0 + GROUP],
                start=(o == 0),
                stop=(o == PASSES - 1),
            )

        def listed(first, width):
            return offsets[:, first // 16 : (first + width) // 16]

        def half_cols(h):
            return slice(h * HALF, (h + 1) * HALF)

        def group_cols(g):
            return slice(g * GROUP, (g + 1) * GROUP)

        round_q(nc.scalar.copy, 0, slice(0, NQ))
        k_picked = [pool.tile([P, HALF], U32, name="k_picked%d" % h, align_bytes=64) for h in range(HALVES)]
        for h in range(HALVES):
            nc.vector.tensor_copy(k_picked[h][:], k_win[:].bitcast(U32).indirect(listed(h * HALF, HALF)))
        k_pass = pool.tile([P, PASSES, N], U16, name="k_pass", align_bytes=64)
        for h in range(HALVES):
            part_passes(k_pass[:, :, half_cols(h)], k_picked[h][:])
        quantize(0)

        kb_flat = kb_win[:].rearrange("m p b -> m (p b)")
        picked_kb = []

        def gather_kb(h):
            at = Q_RAW_AT + Q_RAW_BYTES * h + Q_RAW_BYTES // 2
            picked_kb.append(chain.tile([P, HALF], F32, name="picked_kb%d" % h, offset=at, align_bytes=64))
            nc.scalar.activation(
                picked_kb[h][:], kb_flat.indirect(listed(h * HALF, HALF)), mybir.ActivationFunctionType.Copy
            )

        c_picked = []

        def gather_c(h, at):
            c_picked.append(chain.tile([P, HALF], U32, name="c_picked%d" % h, offset=at, align_bytes=64))
            for lo in range(0, HALF, GROUP):
                nc.vector.tensor_copy(
                    c_picked[h][:, lo : lo + GROUP], c_win[:].bitcast(U32).indirect(listed(h * HALF + lo, GROUP))
                )

        c_pass = pool.tile([P, PASSES, N], U16, name="c_pass", align_bytes=64)
        gather_kb(0)
        gather_c(0, Q_BF_BYTES // 2)
        round_q(nc.scalar.copy, 1, slice(0, NQ // 2))
        round_q(nc.vector.tensor_copy, 1, slice(NQ // 2, NQ))
        part_passes(c_pass[:, :, half_cols(0)], c_picked[0][:])
        quantize(1)
        gather_kb(1)
        gather_c(1, Q_RAW_AT + Q_RAW_BYTES)
        for lo in range(0, HALF, GROUP):
            part_passes(c_pass[:, :, HALF + lo : HALF + lo + GROUP], c_picked[1][:, lo : lo + GROUP])

        a_banks = [psum.tile([NQ, GROUP], F32, name="a_bank%d" % g, tag="bank%d" % g) for g in range(GROUPS)]
        z_banks = [psum.tile([NQ, GROUP], F32, name="z_bank%d" % g, tag="z_bank%d" % g) for g in range(GROUPS)]
        a_sb = [pool.tile([NQ, GROUP], F32, name="a_sb%d" % g, align_bytes=64) for g in range(GROUPS)]
        for g in range(GROUPS):
            score_pass(a_banks[g][:], k_pass, 0, g, 0)
        for pair in ((0, 1), (2, 3)):
            for g in pair:
                score_pass(a_banks[g][:], k_pass, 0, g, 1)
                nc.scalar.copy(a_sb[g][:], a_banks[g][:])
            for g in pair:
                for o in range(PASSES):
                    score_pass(z_banks[g][:], c_pass, 1, g, o)

        best = pool.tile([NQ, N], F32, name="best", align_bytes=64)
        for h, pair in enumerate(((0, 1), (2, 3))):
            for g in pair:
                nc.vector.tensor_tensor(best[:, group_cols(g)], z_banks[g][:], a_sb[g][:], mybir.AluOpType.max)
            for g in pair:
                res = pool.tile([NQ, GROUP], F32, name="res%d" % g, align_bytes=64)
                bias = picked_kb[h][:, group_cols(g % 2)]
                nc.vector.tensor_tensor(res[:], best[:, group_cols(g)], bias, mybir.AluOpType.add)
                nc.sync.dma_start(out[0][:, group_cols(g)], res[:])
